import numpy as np
import ml_dtypes


def mxq(x, axis, fmt="e4m3"):
    dtype, down = {"e4m3": (ml_dtypes.float8_e4m3fn, 7), "e5m2": (ml_dtypes.float8_e5m2, 14)}[fmt]
    v = np.moveaxis(np.asarray(x, np.float32).astype(ml_dtypes.bfloat16).astype(np.float64), axis, -1)
    blocks = v.reshape(v.shape[:-1] + (-1, 32))
    amax = np.abs(blocks).max(-1, keepdims=True)
    byte = np.maximum(np.where(amax > 0, np.frexp(amax)[1] - 1 + 127, 0) - down, 1)
    scale = np.exp2(byte - 127.0)
    codes = (blocks / scale).astype(np.float32).astype(dtype).astype(np.float64)
    return np.moveaxis((codes * scale).reshape(v.shape), -1, axis)


WIDE = False


def mx_kscale(k):
    if not WIDE:
        return np.ones(k)
    levels = np.array([10, -10, 5, -5, 0])
    if k % 512:
        return np.exp2(np.random.permutation(np.resize(levels, k // 32))).repeat(32)
    a = np.empty((k // 512, 16))
    for p in range(k // 512):
        a[p, :8] = np.random.permutation(np.resize(levels, 8))
        for g in range(8):
            far = levels[np.abs(levels - a[p, g]) >= 10]
            a[p, g + 8] = far[np.random.randint(len(far))]
    return np.exp2(a.ravel()).repeat(32)


def f64(x):
    return np.asarray(x).astype(np.float64)


def striped(idx):
    return np.tile(np.asarray(idx).reshape(-1, 16).T, (8, 1)).astype(np.uint16)


def unstriped(offs):
    return offs[:16].T.reshape(-1).astype(np.int64)


E2M1 = np.array([0.0, 0.5, 1.0, 1.5, 2.0, 3.0, 4.0, 6.0, -0.0, -0.5, -1.0, -1.5, -2.0, -3.0, -4.0, -6.0])


def pack_weight(w, fmt):
    k, n = w.shape
    w = f64(np.asarray(w, np.float32).astype(ml_dtypes.bfloat16)).reshape(k // 32, 32, n)
    amax = np.abs(w).max(1)
    if fmt == "e4m3":
        byte = np.frexp(amax)[1] - 1 + 127 - 7
    else:
        mant, ex = np.frexp(amax / 6.0)
        byte = np.where(mant > 0.5, ex, ex - 1) + 127
    byte = np.clip(np.where(amax > 0, byte, 1), 1, 254)
    scaled = (w * np.exp2(127.0 - byte)[:, None, :]).reshape(k, n).astype(np.float32)
    by_word = np.ascontiguousarray(scaled.reshape(k // 512, 128, 4, n).transpose(0, 1, 3, 2))
    if fmt == "e4m3":
        words = by_word.astype(ml_dtypes.float8_e4m3fn).view(np.uint8)
    else:
        c = by_word.astype(ml_dtypes.float4_e2m1fn).view(np.uint8) & 0xF
        words = (c[..., 0::2] | (c[..., 1::2] << 4)).reshape(k // 512, 128, 2 * n)
    return np.ascontiguousarray(words), np.ascontiguousarray(byte.astype(np.uint8).reshape(k // 512, 16, n))


def unpack_weight(words, scales, fmt):
    g, _, n = scales.shape
    words = np.ascontiguousarray(words).reshape(g, 128, n, -1)
    if fmt == "e4m3":
        vals = words.view(ml_dtypes.float8_e4m3fn).astype(np.float64)
    else:
        nib = np.empty((g, 128, n, 4), np.uint8)
        nib[..., 0::2] = words & 0xF
        nib[..., 1::2] = words >> 4
        vals = E2M1[nib]
    vals = vals * np.repeat(np.exp2(scales.astype(np.float64) - 127.0), 8, axis=1)[..., None]
    return vals.transpose(0, 1, 3, 2).reshape(g * 512, n)


B, N, T, D, DV, NQ = 1, 1024, 4096, 512, 0, 128
PAGE = 128
SEG = 128


def setup_inputs():
    n = np.random.standard_normal
    pages = np.random.permutation(T // PAGE)[:B * N // PAGE]
    idx = (pages[:, None] * PAGE + np.arange(PAGE)[None, :]).reshape(-1)
    s = mx_kscale(D)[:, None]
    r = np.random.uniform(0.5, 2.0, T)
    kp = pack_weight(n((D, T)) / s / r, "e4m3")
    return {
        "qT": (n((B, D, NQ)) * s * (1.00 / np.sqrt(D))).astype(np.float32),
        "k_words": kp[0],
        "k_scales": kp[1],
        "ts": np.tile(r, (128, 1)).astype(np.float32),
        "offs": striped(idx),
    }


def reference(qT, k_words, k_scales, ts, offs):
    idx = unstriped(offs)
    pool = unpack_weight(k_words, k_scales, "e4m3")
    pick = lambda x: x[:, idx].reshape(x.shape[0], B, N).transpose(1, 0, 2)
    a = mxq(f64(qT), 1, "e4m3").transpose(0, 2, 1) @ pick(pool)
    a = a * pick(f64(ts))[:, :1, :]
    return a.reshape(B, NQ, N // SEG, SEG).max(-1)

@@ -1,0 +1,126 @@
+from contextlib import ExitStack
+
+import concourse.mybir as mybir
+from concourse.masks import make_identity
+
+F32 = mybir.dt.float32
+BF16 = mybir.dt.bfloat16
+I32 = mybir.dt.int32
+U32 = mybir.dt.uint32
+U16 = mybir.dt.uint16
+U8 = mybir.dt.uint8
+FP8X4 = mybir.dt.float8_e4m3fn_x4
+MULT = mybir.AluOpType.mult
+MAX = mybir.AluOpType.max
+AXIS_X = mybir.AxisListType.X
+
+P = 128
+PACK = 4
+POOL = 4096
+SLOTS = 1024
+QUERIES = 128
+SEG = 128
+PASSAGES = SLOTS // SEG
+HALF = SLOTS // 2
+LIST_COLS = SLOTS // 16
+CHUNK = 256
+TS_ROW = P - 1
+
+FLOPS = 2 * QUERIES * SLOTS * P * PACK
+BYTES = P * POOL * 4 + 16 * POOL + P * PACK * QUERIES * 4 + POOL * 4 + P * LIST_COLS * 2 + QUERIES * PASSAGES * 4
+
+
+def tile_attend_maxsim_ts_kernel(tc, qT, k_words, k_scales, ts, offs, out):
+    nc = tc.nc
+    with ExitStack() as ctx:
+        sb = ctx.enter_context(tc.tile_pool(name="sb", bufs=1))
+        ps = ctx.enter_context(tc.psum_pool(name="ps", bufs=1))
+
+        offsets = sb.tile([P, LIST_COLS], U16, name="offsets")
+        ts_pool = sb.tile([P, POOL], F32, name="ts_pool", align_bytes=64)
+        q_raw = sb.tile([P, PACK, QUERIES], F32, name="q_raw", align_bytes=64)
+        word_pool = sb.tile([P, POOL], I32, name="word_pool", align_bytes=64)
+        scale_pool = sb.tile([P, POOL // 4], I32, name="scale_pool", align_bytes=64)
+        identity = sb.tile([P, P], F32, name="identity", align_bytes=64)
+
+        nc.vector.memset(scale_pool[:], 0)
+        nc.sync.dma_start(offsets[:], offs)
+        nc.sync.dma_start(ts_pool[TS_ROW:P, :], ts[0:1, :])
+        nc.sync.dma_start(q_raw[:], qT[0].rearrange("(p j) w -> p j w", j=PACK))
+        nc.sync.dma_start(word_pool[:], k_words[0].rearrange("p n t -> p (n t)").bitcast(I32))
+        scale_rows = k_scales[0].bitcast(I32)
+        for r in range(4):
+            nc.sync.dma_start(scale_pool[r:P:32, :], scale_rows[r:16:4, :])
+        nc.vector.memset(ts_pool[0:TS_ROW, :], 0.0)
+        make_identity(nc, identity[:])
+
+        halves = [offsets[:, h * LIST_COLS // 2 : (h + 1) * LIST_COLS // 2] for h in range(2)]
+
+        ts_spread = sb.tile([P, SLOTS], F32, name="ts_spread", align_bytes=64)
+        ts_listed = []
+        for h in range(2):
+            t = sb.tile([P, HALF], F32, name="ts_listed%d" % h, align_bytes=64)
+            nc.vector.tensor_copy(t[:], ts_pool[:].indirect(halves[h]))
+            ts_listed.append(t)
+        q_grouped = sb.tile([P, QUERIES, PACK], BF16, name="q_grouped", align_bytes=64)
+        nc.scalar.copy(q_grouped[:], q_raw[:].rearrange("p j w -> p w j"))
+        ts_cols = []
+        for h in range(2):
+            turned = ps.tile([P, 4, SEG], F32, name="turned%d" % h)
+            for j in range(4):
+                nc.tensor.transpose(turned[:, j, :], ts_listed[h][:, j * SEG : (j + 1) * SEG], identity[:])
+            c = sb.tile([P, 4], F32, name="ts_cols%d" % h, align_bytes=64)
+            nc.scalar.copy(c[:], turned[:, :, TS_ROW])
+            ts_cols.append(c)
+        for h in range(2):
+            spread = ps.tile([P, 4, SEG], F32, name="spread%d" % h)
+            for j in range(4):
+                nc.tensor.transpose(spread[:, j, :], ts_cols[h][:, j : j + 1].to_broadcast([P, P]), identity[:])
+            nc.scalar.copy(ts_spread[:, h * HALF : (h + 1) * HALF], spread[:].rearrange("p j s -> p (j s)"))
+
+        q_words = sb.tile([P, QUERIES], U32, name="q_words", align_bytes=64)
+        q_scales = sb.tile([P, QUERIES], U8, name="q_scales", align_bytes=64)
+        nc.vector.quantize_mx(
+            out=q_words[:].bitcast(FP8X4), scales=q_scales[:], in_=q_grouped[:].rearrange("p w j -> p (w j)")
+        )
+
+        key_words = sb.tile([P, SLOTS], U32, name="key_words", align_bytes=64)
+        nc.vector.tensor_copy(key_words[:], word_pool[:].bitcast(U32).indirect(offsets[:]))
+        key_scales = []
+        for h in range(2):
+            s = sb.tile([P, HALF], U8, name="key_scales%d" % h, align_bytes=64)
+            nc.vector.tensor_copy(s[:], scale_pool[:].bitcast(U8).indirect(halves[h]))
+            key_scales.append(s)
+
+        scores = []
+        for c in range(SLOTS // CHUNK):
+            acc = ps.tile([P, CHUNK], F32, name="scores%d" % c)
+            lo = (c % 2) * CHUNK
+            nc.tensor.matmul_mx(
+                out=acc[:],
+                lhsT=q_words[:].bitcast(FP8X4),
+                lhsT_scale=q_scales[:],
+                rhs=key_words[:, c * CHUNK : (c + 1) * CHUNK].bitcast(FP8X4),
+                rhs_scale=key_scales[c // 2][:, lo : lo + CHUNK],
+                start=True,
+                stop=True,
+            )
+            scores.append(acc)
+
+        best = sb.tile([P, PASSAGES], F32, name="best", align_bytes=64)
+        scaled = []
+
+        def reduce_chunk(c):
+            per = CHUNK // SEG
+            nc.vector.tensor_reduce(
+                best[:, c * per : (c + 1) * per], scaled[c][:].rearrange("p (j s) -> p j s", s=SEG), AXIS_X, MAX
+            )
+
+        for c in range(SLOTS // CHUNK):
+            y = sb.tile([P, CHUNK], F32, name="scaled%d" % c, align_bytes=64)
+            nc.vector.tensor_tensor(y[:], scores[c][:], ts_spread[:, c * CHUNK : (c + 1) * CHUNK], MULT)
+            scaled.append(y)
+            if c >= 1:
+                reduce_chunk(c - 1)
+        reduce_chunk(SLOTS // CHUNK - 1)
+        nc.sync.dma_start(out[0], best[:])

@@ -45,12 +45,12 @@ def tile_attend_maxsim_ts_kernel(tc, qT, k_words, k_scales, ts, offs, out):
 
         nc.vector.memset(scale_pool[:], 0)
         nc.sync.dma_start(offsets[:], offs)
-        nc.sync.dma_start(ts_pool[TS_ROW:P, :], ts[0:1, :])
-        nc.sync.dma_start(q_raw[:], qT[0].rearrange("(p j) w -> p j w", j=PACK))
-        nc.sync.dma_start(word_pool[:], k_words[0].rearrange("p n t -> p (n t)").bitcast(I32))
+        nc.scalar.dma_start(q_raw[:], qT[0].rearrange("(p j) w -> p j w", j=PACK))
+        nc.scalar.dma_start(ts_pool[TS_ROW:P, :], ts[0:1, :])
         scale_rows = k_scales[0].bitcast(I32)
         for r in range(4):
             nc.sync.dma_start(scale_pool[r:P:32, :], scale_rows[r:16:4, :])
+        nc.sync.dma_start(word_pool[:], k_words[0].rearrange("p n t -> p (n t)").bitcast(I32))
         nc.vector.memset(ts_pool[0:TS_ROW, :], 0.0)
         make_identity(nc, identity[:])
 
@@ -84,13 +84,13 @@ def tile_attend_maxsim_ts_kernel(tc, qT, k_words, k_scales, ts, offs, out):
             out=q_words[:].bitcast(FP8X4), scales=q_scales[:], in_=q_grouped[:].rearrange("p w j -> p (w j)")
         )
 
-        key_words = sb.tile([P, SLOTS], U32, name="key_words", align_bytes=64)
-        nc.vector.tensor_copy(key_words[:], word_pool[:].bitcast(U32).indirect(offsets[:]))
-        key_scales = []
+        key_scales = sb.tile([P, SLOTS], U8, name="key_scales", align_bytes=64)
+        nc.vector.tensor_copy(key_scales[:], scale_pool[:].bitcast(U8).indirect(offsets[:]))
+        key_words = []
         for h in range(2):
-            s = sb.tile([P, HALF], U8, name="key_scales%d" % h, align_bytes=64)
-            nc.vector.tensor_copy(s[:], scale_pool[:].bitcast(U8).indirect(halves[h]))
-            key_scales.append(s)
+            w = sb.tile([P, HALF], U32, name="key_words%d" % h, align_bytes=64)
+            nc.vector.tensor_copy(w[:], word_pool[:].bitcast(U32).indirect(halves[h]))
+            key_words.append(w)
 
         scores = []
         for c in range(SLOTS // CHUNK):
@@ -100,8 +100,8 @@ def tile_attend_maxsim_ts_kernel(tc, qT, k_words, k_scales, ts, offs, out):
                 out=acc[:],
                 lhsT=q_words[:].bitcast(FP8X4),
                 lhsT_scale=q_scales[:],
-                rhs=key_words[:, c * CHUNK : (c + 1) * CHUNK].bitcast(FP8X4),
-                rhs_scale=key_scales[c // 2][:, lo : lo + CHUNK],
+                rhs=key_words[c // 2][:, lo : lo + CHUNK].bitcast(FP8X4),
+                rhs_scale=key_scales[:, c * CHUNK : (c + 1) * CHUNK],
                 start=True,
                 stop=True,
             )

@@ -46,7 +46,7 @@ def tile_attend_maxsim_ts_kernel(tc, qT, k_words, k_scales, ts, offs, out):
         nc.vector.memset(scale_pool[:], 0)
         nc.sync.dma_start(offsets[:], offs)
         nc.scalar.dma_start(q_raw[:], qT[0].rearrange("(p j) w -> p j w", j=PACK))
-        nc.scalar.dma_start(ts_pool[TS_ROW:P, :], ts[0:1, :])
+        nc.sync.dma_start(ts_pool[TS_ROW:P, :], ts[0:1, :])
         scale_rows = k_scales[0].bitcast(I32)
         for r in range(4):
             nc.sync.dma_start(scale_pool[r:P:32, :], scale_rows[r:16:4, :])
@@ -57,11 +57,20 @@ def tile_attend_maxsim_ts_kernel(tc, qT, k_words, k_scales, ts, offs, out):
         halves = [offsets[:, h * LIST_COLS // 2 : (h + 1) * LIST_COLS // 2] for h in range(2)]
 
         ts_spread = sb.tile([P, SLOTS], F32, name="ts_spread", align_bytes=64)
-        ts_listed = []
-        for h in range(2):
-            t = sb.tile([P, HALF], F32, name="ts_listed%d" % h, align_bytes=64)
-            nc.vector.tensor_copy(t[:], ts_pool[:].indirect(halves[h]))
-            ts_listed.append(t)
+        ones = sb.tile([P, 2 * SEG], F32, name="ones", align_bytes=64)
+        nc.scalar.activation(
+            ones[:].rearrange("p (a b) -> p a b", a=2),
+            identity[:].unsqueeze(1).to_broadcast([P, 2, P]),
+            mybir.ActivationFunctionType.Copy,
+            bias=1.0,
+            scale=0.0,
+        )
+        ts_listed = [sb.tile([P, HALF], F32, name="ts_listed%d" % h, align_bytes=64) for h in range(2)]
+        for lo, hi in ((0, SEG), (SEG, 2 * SEG), (2 * SEG, HALF)):
+            nc.vector.tensor_tensor(
+                ts_listed[0][:, lo:hi], ts_pool[:].indirect(offsets[:, lo // 16 : hi // 16]), ones[:, 0 : hi - lo], MULT
+            )
+        nc.vector.tensor_copy(ts_listed[1][:], ts_pool[:].indirect(halves[1]))
         q_grouped = sb.tile([P, QUERIES, PACK], BF16, name="q_grouped", align_bytes=64)
         nc.scalar.copy(q_grouped[:], q_raw[:].rearrange("p j w -> p w j"))
         ts_cols = []

@@ -25,6 +25,7 @@ HALF = SLOTS // 2
 LIST_COLS = SLOTS // 16
 CHUNK = 256
 TS_ROW = P - 1
+SCALE_ROW = 48
 
 FLOPS = 2 * QUERIES * SLOTS * P * PACK
 BYTES = P * POOL * 4 + 16 * POOL + P * PACK * QUERIES * 4 + POOL * 4 + P * LIST_COLS * 2 + QUERIES * PASSAGES * 4
@@ -40,76 +41,73 @@ def tile_attend_maxsim_ts_kernel(tc, qT, k_words, k_scales, ts, offs, out):
         ts_pool = sb.tile([P, POOL], F32, name="ts_pool", align_bytes=64)
         q_raw = sb.tile([P, PACK, QUERIES], F32, name="q_raw", align_bytes=64)
         word_pool = sb.tile([P, POOL], I32, name="word_pool", align_bytes=64)
-        scale_pool = sb.tile([P, POOL // 4], I32, name="scale_pool", align_bytes=64)
+        scale_pool = sb.tile([P, POOL // 4], I32, name="scale_pool", tag="scales_then_words", align_bytes=64)
+        key_plane = sb.tile([P, SLOTS // 4], I32, name="key_plane", align_bytes=64)
         identity = sb.tile([P, P], F32, name="identity", align_bytes=64)
 
-        nc.vector.memset(scale_pool[:], 0)
+        nc.sync.dma_start(ts_pool[TS_ROW:P, :], ts[0:1, :])
         nc.sync.dma_start(offsets[:], offs)
         nc.scalar.dma_start(q_raw[:], qT[0].rearrange("(p j) w -> p j w", j=PACK))
-        nc.sync.dma_start(ts_pool[TS_ROW:P, :], ts[0:1, :])
-        scale_rows = k_scales[0].bitcast(I32)
-        for r in range(4):
-            nc.sync.dma_start(scale_pool[r:P:32, :], scale_rows[r:16:4, :])
-        nc.sync.dma_start(word_pool[:], k_words[0].rearrange("p n t -> p (n t)").bitcast(I32))
-        nc.vector.memset(ts_pool[0:TS_ROW, :], 0.0)
+        nc.scalar.dma_start(scale_pool[SCALE_ROW : SCALE_ROW + 16, :], k_scales[0].bitcast(I32))
+        nc.scalar.dma_start(word_pool[:], k_words[0].rearrange("p n t -> p (n t)").bitcast(I32))
+
         make_identity(nc, identity[:])
+        nc.vector.memset(ts_pool[0:TS_ROW, 0:1023], 0.0)
+        nc.vector.memset(ts_pool[0:TS_ROW, 1023:2048], 0.0)
+        nc.gpsimd.memset(ts_pool[0:TS_ROW, 2048:POOL], 0.0)
+        nc.gpsimd.memset(scale_pool[0:SCALE_ROW, :], 0)
+        nc.gpsimd.memset(scale_pool[SCALE_ROW + 16 : P, :], 0)
+        nc.gpsimd.memset(key_plane[:], 0)
 
         halves = [offsets[:, h * LIST_COLS // 2 : (h + 1) * LIST_COLS // 2] for h in range(2)]
 
-        ts_spread = sb.tile([P, SLOTS], F32, name="ts_spread", align_bytes=64)
-        ones = sb.tile([P, 2 * SEG], F32, name="ones", align_bytes=64)
-        nc.scalar.activation(
-            ones[:].rearrange("p (a b) -> p a b", a=2),
-            identity[:].unsqueeze(1).to_broadcast([P, 2, P]),
-            mybir.ActivationFunctionType.Copy,
-            bias=1.0,
-            scale=0.0,
-        )
         ts_listed = [sb.tile([P, HALF], F32, name="ts_listed%d" % h, align_bytes=64) for h in range(2)]
-        for lo, hi in ((0, SEG), (SEG, 2 * SEG), (2 * SEG, HALF)):
-            nc.vector.tensor_tensor(
-                ts_listed[0][:, lo:hi], ts_pool[:].indirect(offsets[:, lo // 16 : hi // 16]), ones[:, 0 : hi - lo], MULT
-            )
-        nc.vector.tensor_copy(ts_listed[1][:], ts_pool[:].indirect(halves[1]))
+        for h in range(2):
+            nc.vector.tensor_copy(ts_listed[h][:], ts_pool[:].indirect(halves[h]))
         q_grouped = sb.tile([P, QUERIES, PACK], BF16, name="q_grouped", align_bytes=64)
         nc.scalar.copy(q_grouped[:], q_raw[:].rearrange("p j w -> p w j"))
-        ts_cols = []
-        for h in range(2):
-            turned = ps.tile([P, 4, SEG], F32, name="turned%d" % h)
-            for j in range(4):
-                nc.tensor.transpose(turned[:, j, :], ts_listed[h][:, j * SEG : (j + 1) * SEG], identity[:])
-            c = sb.tile([P, 4], F32, name="ts_cols%d" % h, align_bytes=64)
-            nc.scalar.copy(c[:], turned[:, :, TS_ROW])
-            ts_cols.append(c)
-        for h in range(2):
-            spread = ps.tile([P, 4, SEG], F32, name="spread%d" % h)
-            for j in range(4):
-                nc.tensor.transpose(spread[:, j, :], ts_cols[h][:, j : j + 1].to_broadcast([P, P]), identity[:])
-            nc.scalar.copy(ts_spread[:, h * HALF : (h + 1) * HALF], spread[:].rearrange("p j s -> p (j s)"))
-
         q_words = sb.tile([P, QUERIES], U32, name="q_words", align_bytes=64)
         q_scales = sb.tile([P, QUERIES], U8, name="q_scales", align_bytes=64)
         nc.vector.quantize_mx(
             out=q_words[:].bitcast(FP8X4), scales=q_scales[:], in_=q_grouped[:].rearrange("p w j -> p (w j)")
         )
 
-        key_scales = sb.tile([P, SLOTS], U8, name="key_scales", align_bytes=64)
-        nc.vector.tensor_copy(key_scales[:], scale_pool[:].bitcast(U8).indirect(offsets[:]))
-        key_words = []
+        ts_spread = sb.tile([P, SLOTS], F32, name="ts_spread", align_bytes=64)
         for h in range(2):
-            w = sb.tile([P, HALF], U32, name="key_words%d" % h, align_bytes=64)
-            nc.vector.tensor_copy(w[:], word_pool[:].bitcast(U32).indirect(halves[h]))
-            key_words.append(w)
+            turned = ps.tile([P, 4, SEG], F32, name="turned%d" % h)
+            for j in range(4):
+                nc.tensor.transpose(turned[:, j, :], ts_listed[h][:, j * SEG : (j + 1) * SEG], identity[:])
+            cols = sb.tile([P, 4], F32, name="ts_cols%d" % h, align_bytes=64)
+            nc.scalar.copy(cols[:], turned[:, :, TS_ROW])
+            spread = ps.tile([P, 4, SEG], F32, name="spread%d" % h)
+            for j in range(4):
+                nc.tensor.transpose(spread[:, j, :], cols[:, j : j + 1].to_broadcast([P, P]), identity[:])
+            nc.scalar.copy(ts_spread[:, h * HALF : (h + 1) * HALF], spread[:].rearrange("p j s -> p (j s)"))
+
+        for h in range(2):
+            listed = sb.tile([P, HALF // 4], I32, name="scales_listed%d" % h, align_bytes=64)
+            nc.vector.tensor_copy(listed[:].bitcast(U8), scale_pool[:].bitcast(U8).indirect(halves[h]))
+            for quad in range(4):
+                nc.sync.dma_start(
+                    key_plane[32 * quad : 32 * quad + 4, h * HALF // 4 : (h + 1) * HALF // 4],
+                    listed[SCALE_ROW + 4 * quad : SCALE_ROW + 4 * quad + 4, :],
+                )
+        key_scales = key_plane[:].bitcast(U8)
+
+        key_words = sb.tile([P, SLOTS], U32, name="key_words", tag="scales_then_words", align_bytes=64)
+        for h in range(2):
+            nc.vector.tensor_copy(
+                key_words[:, h * HALF : (h + 1) * HALF], word_pool[:].bitcast(U32).indirect(halves[h])
+            )
 
         scores = []
         for c in range(SLOTS // CHUNK):
             acc = ps.tile([P, CHUNK], F32, name="scores%d" % c)
-            lo = (c % 2) * CHUNK
             nc.tensor.matmul_mx(
                 out=acc[:],
                 lhsT=q_words[:].bitcast(FP8X4),
                 lhsT_scale=q_scales[:],
-                rhs=key_words[c // 2][:, lo : lo + CHUNK].bitcast(FP8X4),
+                rhs=key_words[:, c * CHUNK : (c + 1) * CHUNK].bitcast(FP8X4),
                 rhs_scale=key_scales[:, c * CHUNK : (c + 1) * CHUNK],
                 start=True,
                 stop=True,

@@ -25,7 +25,7 @@ HALF = SLOTS // 2
 LIST_COLS = SLOTS // 16
 CHUNK = 256
 TS_ROW = P - 1
-SCALE_ROW = 48
+SCALE_ROW = P - 16
 
 FLOPS = 2 * QUERIES * SLOTS * P * PACK
 BYTES = P * POOL * 4 + 16 * POOL + P * PACK * QUERIES * 4 + POOL * 4 + P * LIST_COLS * 2 + QUERIES * PASSAGES * 4
@@ -51,12 +51,11 @@ def tile_attend_maxsim_ts_kernel(tc, qT, k_words, k_scales, ts, offs, out):
         nc.scalar.dma_start(scale_pool[SCALE_ROW : SCALE_ROW + 16, :], k_scales[0].bitcast(I32))
         nc.scalar.dma_start(word_pool[:], k_words[0].rearrange("p n t -> p (n t)").bitcast(I32))
 
+        nc.vector.memset(ts_pool[0:TS_ROW, 0:879], 0.0)
+        nc.vector.memset(ts_pool[0:TS_ROW, 879:1760], 0.0)
+        nc.gpsimd.memset(ts_pool[0:TS_ROW, 1760:POOL], 0.0)
         make_identity(nc, identity[:])
-        nc.vector.memset(ts_pool[0:TS_ROW, 0:1023], 0.0)
-        nc.vector.memset(ts_pool[0:TS_ROW, 1023:2048], 0.0)
-        nc.gpsimd.memset(ts_pool[0:TS_ROW, 2048:POOL], 0.0)
         nc.gpsimd.memset(scale_pool[0:SCALE_ROW, :], 0)
-        nc.gpsimd.memset(scale_pool[SCALE_ROW + 16 : P, :], 0)
         nc.gpsimd.memset(key_plane[:], 0)
 
         halves = [offsets[:, h * LIST_COLS // 2 : (h + 1) * LIST_COLS // 2] for h in range(2)]

@@ -41,8 +41,8 @@ def tile_attend_maxsim_ts_kernel(tc, qT, k_words, k_scales, ts, offs, out):
         ts_pool = sb.tile([P, POOL], F32, name="ts_pool", align_bytes=64)
         q_raw = sb.tile([P, PACK, QUERIES], F32, name="q_raw", align_bytes=64)
         word_pool = sb.tile([P, POOL], I32, name="word_pool", align_bytes=64)
-        scale_pool = sb.tile([P, POOL // 4], I32, name="scale_pool", tag="scales_then_words", align_bytes=64)
-        key_plane = sb.tile([P, SLOTS // 4], I32, name="key_plane", align_bytes=64)
+        scale_pool = sb.tile([P, POOL // 4], I32, name="scale_pool", align_bytes=64)
+        planes = sb.tile([P, (SLOTS + QUERIES) // 4], I32, name="planes", align_bytes=64)
         identity = sb.tile([P, P], F32, name="identity", align_bytes=64)
 
         nc.sync.dma_start(ts_pool[TS_ROW:P, :], ts[0:1, :])
@@ -56,19 +56,19 @@ def tile_attend_maxsim_ts_kernel(tc, qT, k_words, k_scales, ts, offs, out):
         nc.gpsimd.memset(ts_pool[0:TS_ROW, 1760:POOL], 0.0)
         make_identity(nc, identity[:])
         nc.gpsimd.memset(scale_pool[0:SCALE_ROW, :], 0)
-        nc.gpsimd.memset(key_plane[:], 0)
+        nc.gpsimd.memset(planes[:], 0)
 
         halves = [offsets[:, h * LIST_COLS // 2 : (h + 1) * LIST_COLS // 2] for h in range(2)]
 
         ts_listed = [sb.tile([P, HALF], F32, name="ts_listed%d" % h, align_bytes=64) for h in range(2)]
         for h in range(2):
             nc.vector.tensor_copy(ts_listed[h][:], ts_pool[:].indirect(halves[h]))
-        q_grouped = sb.tile([P, QUERIES, PACK], BF16, name="q_grouped", align_bytes=64)
+        q_grouped = sb.tile([P, QUERIES, PACK], BF16, name="q_grouped", tag="queries_then_words", align_bytes=64)
         nc.scalar.copy(q_grouped[:], q_raw[:].rearrange("p j w -> p w j"))
         q_words = sb.tile([P, QUERIES], U32, name="q_words", align_bytes=64)
-        q_scales = sb.tile([P, QUERIES], U8, name="q_scales", align_bytes=64)
+        q_scales = planes[:, SLOTS // 4 :].bitcast(U8)
         nc.vector.quantize_mx(
-            out=q_words[:].bitcast(FP8X4), scales=q_scales[:], in_=q_grouped[:].rearrange("p w j -> p (w j)")
+            out=q_words[:].bitcast(FP8X4), scales=q_scales, in_=q_grouped[:].rearrange("p w j -> p (w j)")
         )
 
         ts_spread = sb.tile([P, SLOTS], F32, name="ts_spread", align_bytes=64)
@@ -88,12 +88,12 @@ def tile_attend_maxsim_ts_kernel(tc, qT, k_words, k_scales, ts, offs, out):
             nc.vector.tensor_copy(listed[:].bitcast(U8), scale_pool[:].bitcast(U8).indirect(halves[h]))
             for quad in range(4):
                 nc.sync.dma_start(
-                    key_plane[32 * quad : 32 * quad + 4, h * HALF // 4 : (h + 1) * HALF // 4],
+                    planes[32 * quad : 32 * quad + 4, h * HALF // 4 : (h + 1) * HALF // 4],
                     listed[SCALE_ROW + 4 * quad : SCALE_ROW + 4 * quad + 4, :],
                 )
-        key_scales = key_plane[:].bitcast(U8)
+        key_scales = planes[:, 0 : SLOTS // 4].bitcast(U8)
 
-        key_words = sb.tile([P, SLOTS], U32, name="key_words", tag="scales_then_words", align_bytes=64)
+        key_words = sb.tile([P, SLOTS], U32, name="key_words", tag="queries_then_words", align_bytes=64)
         for h in range(2):
             nc.vector.tensor_copy(
                 key_words[:, h * HALF : (h + 1) * HALF], word_pool[:].bitcast(U32).indirect(halves[h])
@@ -105,7 +105,7 @@ def tile_attend_maxsim_ts_kernel(tc, qT, k_words, k_scales, ts, offs, out):
             nc.tensor.matmul_mx(
                 out=acc[:],
                 lhsT=q_words[:].bitcast(FP8X4),
-                lhsT_scale=q_scales[:],
+                lhsT_scale=q_scales,
                 rhs=key_words[:, c * CHUNK : (c + 1) * CHUNK].bitcast(FP8X4),
                 rhs_scale=key_scales[:, c * CHUNK : (c + 1) * CHUNK],
                 start=True,

@@ -13,6 +13,7 @@ FP8X4 = mybir.dt.float8_e4m3fn_x4
 MULT = mybir.AluOpType.mult
 MAX = mybir.AluOpType.max
 AXIS_X = mybir.AxisListType.X
+COPY = mybir.ActivationFunctionType.Copy
 
 P = 128
 PACK = 4
@@ -35,6 +36,7 @@ def tile_attend_maxsim_ts_kernel(tc, qT, k_words, k_scales, ts, offs, out):
     nc = tc.nc
     with ExitStack() as ctx:
         sb = ctx.enter_context(tc.tile_pool(name="sb", bufs=1))
+        shared = ctx.enter_context(tc.tile_pool(name="shared", bufs=1))
         ps = ctx.enter_context(tc.psum_pool(name="ps", bufs=1))
 
         offsets = sb.tile([P, LIST_COLS], U16, name="offsets")
@@ -54,16 +56,21 @@ def tile_attend_maxsim_ts_kernel(tc, qT, k_words, k_scales, ts, offs, out):
         nc.vector.memset(ts_pool[0:TS_ROW, 0:879], 0.0)
         nc.vector.memset(ts_pool[0:TS_ROW, 879:1760], 0.0)
         nc.gpsimd.memset(ts_pool[0:TS_ROW, 1760:POOL], 0.0)
-        make_identity(nc, identity[:])
         nc.gpsimd.memset(scale_pool[0:SCALE_ROW, :], 0)
+        make_identity(nc, identity[:])
         nc.gpsimd.memset(planes[:], 0)
 
         halves = [offsets[:, h * LIST_COLS // 2 : (h + 1) * LIST_COLS // 2] for h in range(2)]
 
         ts_listed = [sb.tile([P, HALF], F32, name="ts_listed%d" % h, align_bytes=64) for h in range(2)]
-        for h in range(2):
-            nc.vector.tensor_copy(ts_listed[h][:], ts_pool[:].indirect(halves[h]))
-        q_grouped = sb.tile([P, QUERIES, PACK], BF16, name="q_grouped", tag="queries_then_words", align_bytes=64)
+        nc.vector.tensor_copy(ts_listed[1][:], ts_pool[:].indirect(halves[1]))
+        scales_listed = [
+            shared.tile([P, HALF // 4], I32, name="scales_listed%d" % h, align_bytes=64, offset=(1024, 0)[h])
+            for h in range(2)
+        ]
+        nc.vector.tensor_copy(scales_listed[0][:].bitcast(U8), scale_pool[:].bitcast(U8).indirect(halves[0]))
+
+        q_grouped = shared.tile([P, QUERIES, PACK], BF16, name="q_grouped", align_bytes=64, offset=0)
         nc.scalar.copy(q_grouped[:], q_raw[:].rearrange("p j w -> p w j"))
         q_words = sb.tile([P, QUERIES], U32, name="q_words", align_bytes=64)
         q_scales = planes[:, SLOTS // 4 :].bitcast(U8)
@@ -71,62 +78,104 @@ def tile_attend_maxsim_ts_kernel(tc, qT, k_words, k_scales, ts, offs, out):
             out=q_words[:].bitcast(FP8X4), scales=q_scales, in_=q_grouped[:].rearrange("p w j -> p (w j)")
         )
 
-        ts_spread = sb.tile([P, SLOTS], F32, name="ts_spread", align_bytes=64)
-        for h in range(2):
-            turned = ps.tile([P, 4, SEG], F32, name="turned%d" % h)
-            for j in range(4):
-                nc.tensor.transpose(turned[:, j, :], ts_listed[h][:, j * SEG : (j + 1) * SEG], identity[:])
-            cols = sb.tile([P, 4], F32, name="ts_cols%d" % h, align_bytes=64)
-            nc.scalar.copy(cols[:], turned[:, :, TS_ROW])
-            spread = ps.tile([P, 4, SEG], F32, name="spread%d" % h)
-            for j in range(4):
-                nc.tensor.transpose(spread[:, j, :], cols[:, j : j + 1].to_broadcast([P, P]), identity[:])
-            nc.scalar.copy(ts_spread[:, h * HALF : (h + 1) * HALF], spread[:].rearrange("p j s -> p (j s)"))
+        scales_dealt = sb.tile([P, HALF // 4], I32, name="scales_dealt", align_bytes=64)
+        nc.vector.tensor_copy(
+            scales_dealt[:].rearrange("p (k j w) -> p k j w", k=2, j=4),
+            scales_listed[0][:].rearrange("p (j k w) -> p k j w", k=2, j=4),
+        )
+        nc.vector.tensor_copy(scales_listed[1][:].bitcast(U8), scale_pool[:].bitcast(U8).indirect(halves[1]))
+        nc.vector.tensor_copy(ts_listed[0][:], ts_pool[:].indirect(halves[0]))
 
-        for h in range(2):
-            listed = sb.tile([P, HALF // 4], I32, name="scales_listed%d" % h, align_bytes=64)
-            nc.vector.tensor_copy(listed[:].bitcast(U8), scale_pool[:].bitcast(U8).indirect(halves[h]))
+        turned1 = ps.tile([P, 4, SEG], F32, name="turned1", tag="bank0")
+        for j in range(4):
+            nc.tensor.transpose(turned1[:, j, :], ts_listed[1][:, j * SEG : (j + 1) * SEG], identity[:])
+        ts_cols1 = sb.tile([P, 4], F32, name="ts_cols1", align_bytes=64)
+        nc.scalar.copy(ts_cols1[:], turned1[:, :, TS_ROW])
+        spread = ps.tile([P, 4, SEG], F32, name="spread", tag="bank1")
+        for j in range(4):
+            nc.tensor.transpose(spread[:, j, :], ts_cols1[:, j : j + 1].to_broadcast([P, P]), identity[:])
+        ts_spread = sb.tile([P, HALF], F32, name="ts_spread", align_bytes=64)
+        nc.scalar.copy(ts_spread[:], spread[:].rearrange("p j s -> p (j s)"))
+        ts_dealt = sb.tile([P, HALF], F32, name="ts_dealt", align_bytes=64)
+        nc.scalar.copy(
+            ts_dealt[:].rearrange("p (k j s) -> p k j s", k=2, j=4),
+            ts_listed[0][:].rearrange("p (j k s) -> p k j s", k=2, j=4),
+        )
+        turned0 = ps.tile([P, 4, SEG], F32, name="turned0", tag="bank2")
+        for j in range(4):
+            nc.tensor.transpose(turned0[:, j, :], ts_dealt[:, j * SEG : (j + 1) * SEG], identity[:])
+        ts_cols0 = sb.tile([P, 4], F32, name="ts_cols0", align_bytes=64)
+        nc.scalar.copy(ts_cols0[:], turned0[:, :, TS_ROW])
+
+        for h, moved in enumerate((scales_dealt, scales_listed[1])):
             for quad in range(4):
                 nc.sync.dma_start(
                     planes[32 * quad : 32 * quad + 4, h * HALF // 4 : (h + 1) * HALF // 4],
-                    listed[SCALE_ROW + 4 * quad : SCALE_ROW + 4 * quad + 4, :],
+                    moved[SCALE_ROW + 4 * quad : SCALE_ROW + 4 * quad + 4, :],
                 )
         key_scales = planes[:, 0 : SLOTS // 4].bitcast(U8)
 
-        key_words = sb.tile([P, SLOTS], U32, name="key_words", tag="queries_then_words", align_bytes=64)
-        for h in range(2):
-            nc.vector.tensor_copy(
-                key_words[:, h * HALF : (h + 1) * HALF], word_pool[:].bitcast(U32).indirect(halves[h])
+        key_words = shared.tile([P, SLOTS], U32, name="key_words", align_bytes=64, offset=512)
+        nc.vector.tensor_copy(
+            key_words[:, 0:HALF].rearrange("p (k j s) -> p j k s", k=2, j=4),
+            word_pool[:].bitcast(U32).indirect(halves[0]),
+        )
+        nc.vector.tensor_copy(key_words[:, HALF:SLOTS], word_pool[:].bitcast(U32).indirect(halves[1]))
+
+        def by_slot(acc, t):
+            nc.tensor.matmul_mx(
+                out=acc,
+                lhsT=key_words[:, t * SEG : (t + 1) * SEG].bitcast(FP8X4),
+                lhsT_scale=key_scales[:, t * SEG : (t + 1) * SEG],
+                rhs=q_words[:].bitcast(FP8X4),
+                rhs_scale=q_scales,
+                start=True,
+                stop=True,
             )
 
+        lower = []
+        for a in range(2):
+            acc = ps.tile([P, QUERIES], F32, name="lower%d" % a, tag="bank%d" % a)
+            by_slot(acc[:], a)
+            y = sb.tile([P, QUERIES], F32, name="lower_scaled%d" % a, align_bytes=64)
+            nc.scalar.activation(y[:], acc[:], COPY, scale=ts_cols0[:, a : a + 1])
+            lower.append(y)
+        upper = ps.tile([P, 2, QUERIES], F32, name="upper", tag="bank2")
+        for a in range(2):
+            by_slot(upper[:, a, :], 2 + a)
+
+        widths = (SEG, SEG, 2 * SEG)
         scores = []
-        for c in range(SLOTS // CHUNK):
-            acc = ps.tile([P, CHUNK], F32, name="scores%d" % c)
+        at = HALF
+        for c, width in enumerate(widths):
+            acc = ps.tile([P, width], F32, name="scores%d" % c)
             nc.tensor.matmul_mx(
                 out=acc[:],
                 lhsT=q_words[:].bitcast(FP8X4),
                 lhsT_scale=q_scales,
-                rhs=key_words[:, c * CHUNK : (c + 1) * CHUNK].bitcast(FP8X4),
-                rhs_scale=key_scales[:, c * CHUNK : (c + 1) * CHUNK],
+                rhs=key_words[:, at : at + width].bitcast(FP8X4),
+                rhs_scale=key_scales[:, at : at + width],
                 start=True,
                 stop=True,
             )
             scores.append(acc)
+            at = at + width
+
+        folded = []
+        for a in range(2):
+            z = sb.tile([P, QUERIES], F32, name="folded%d" % a, align_bytes=64)
+            nc.vector.scalar_tensor_tensor(z[:], upper[:, a, :], ts_cols0[:, 2 + a : 3 + a], lower[a][:], MULT, MAX)
+            folded.append(z)
+        back = ps.tile([P, 2, P], F32, name="back")
+        for a in range(2):
+            nc.tensor.transpose(back[:, a, :], folded[a][:], identity[:])
 
         best = sb.tile([P, PASSAGES], F32, name="best", align_bytes=64)
-        scaled = []
-
-        def reduce_chunk(c):
-            per = CHUNK // SEG
-            nc.vector.tensor_reduce(
-                best[:, c * per : (c + 1) * per], scaled[c][:].rearrange("p (j s) -> p j s", s=SEG), AXIS_X, MAX
-            )
-
-        for c in range(SLOTS // CHUNK):
-            y = sb.tile([P, CHUNK], F32, name="scaled%d" % c, align_bytes=64)
-            nc.vector.tensor_tensor(y[:], scores[c][:], ts_spread[:, c * CHUNK : (c + 1) * CHUNK], MULT)
-            scaled.append(y)
-            if c >= 1:
-                reduce_chunk(c - 1)
-        reduce_chunk(SLOTS // CHUNK - 1)
+        scaled = [sb.tile([P, CHUNK], F32, name="scaled%d" % c, align_bytes=64) for c in range(2)]
+        nc.vector.tensor_tensor(scaled[0][:, 0:SEG], scores[0][:], ts_spread[:, 0:SEG], MULT)
+        nc.vector.tensor_tensor(scaled[0][:, SEG:CHUNK], scores[1][:], ts_spread[:, SEG:CHUNK], MULT)
+        nc.vector.tensor_tensor(scaled[1][:], scores[2][:], ts_spread[:, CHUNK:HALF], MULT)
+        nc.vector.tensor_reduce(best[:, 4:6], scaled[0][:].rearrange("p (j s) -> p j s", s=SEG), AXIS_X, MAX)
+        nc.vector.tensor_reduce(best[:, 6:8], scaled[1][:].rearrange("p (j s) -> p j s", s=SEG), AXIS_X, MAX)
+        nc.vector.tensor_reduce(best[:, 0:4], back[:].rearrange("p a (j s) -> p (a j) s", j=2), AXIS_X, MAX)
         nc.sync.dma_start(out[0], best[:])

@@ -22,9 +22,9 @@ SLOTS = 1024
 QUERIES = 128
 SEG = 128
 PASSAGES = SLOTS // SEG
-HALF = SLOTS // 2
 LIST_COLS = SLOTS // 16
-CHUNK = 256
+PIECES = 4
+PIECE = SLOTS // PIECES
 TS_ROW = P - 1
 SCALE_ROW = P - 16
 
@@ -43,139 +43,94 @@ def tile_attend_maxsim_ts_kernel(tc, qT, k_words, k_scales, ts, offs, out):
         ts_pool = sb.tile([P, POOL], F32, name="ts_pool", align_bytes=64)
         q_raw = sb.tile([P, PACK, QUERIES], F32, name="q_raw", align_bytes=64)
         word_pool = sb.tile([P, POOL], I32, name="word_pool", align_bytes=64)
-        scale_pool = sb.tile([P, POOL // 4], I32, name="scale_pool", align_bytes=64)
-        planes = sb.tile([P, (SLOTS + QUERIES) // 4], I32, name="planes", align_bytes=64)
+        scale_pool = shared.tile([P, POOL // 4], I32, name="scale_pool", align_bytes=64, offset=0)
+        planes = sb.tile([P, SLOTS // 4], I32, name="planes", align_bytes=64)
         identity = sb.tile([P, P], F32, name="identity", align_bytes=64)
 
-        nc.sync.dma_start(ts_pool[TS_ROW:P, :], ts[0:1, :])
         nc.sync.dma_start(offsets[:], offs)
+        nc.sync.dma_start(ts_pool[TS_ROW:P, :], ts[0:1, :])
         nc.scalar.dma_start(q_raw[:], qT[0].rearrange("(p j) w -> p j w", j=PACK))
-        nc.scalar.dma_start(scale_pool[SCALE_ROW : SCALE_ROW + 16, :], k_scales[0].bitcast(I32))
+        nc.scalar.dma_start(scale_pool[SCALE_ROW:P, :], k_scales[0].bitcast(I32))
         nc.scalar.dma_start(word_pool[:], k_words[0].rearrange("p n t -> p (n t)").bitcast(I32))
 
-        nc.vector.memset(ts_pool[0:TS_ROW, 0:879], 0.0)
-        nc.vector.memset(ts_pool[0:TS_ROW, 879:1760], 0.0)
-        nc.gpsimd.memset(ts_pool[0:TS_ROW, 1760:POOL], 0.0)
-        nc.gpsimd.memset(scale_pool[0:SCALE_ROW, :], 0)
         make_identity(nc, identity[:])
+        nc.vector.memset(ts_pool[0:TS_ROW, 0:1151], 0.0)
+        nc.vector.memset(ts_pool[0:TS_ROW, 1151:2304], 0.0)
+        nc.gpsimd.memset(ts_pool[0:TS_ROW, 2304:2560], 0.0)
+        nc.gpsimd.memset(ts_pool[0:TS_ROW, 2560:POOL], 0.0)
+        nc.vector.memset(scale_pool[0:SCALE_ROW, 0:255], 0)
+        nc.vector.memset(scale_pool[0:SCALE_ROW, 255:512], 0)
+        nc.gpsimd.memset(scale_pool[0:SCALE_ROW, 512 : POOL // 4], 0)
         nc.gpsimd.memset(planes[:], 0)
 
-        halves = [offsets[:, h * LIST_COLS // 2 : (h + 1) * LIST_COLS // 2] for h in range(2)]
+        cols = LIST_COLS // PIECES
+        pieces = [offsets[:, k * cols : (k + 1) * cols] for k in range(PIECES)]
 
-        ts_listed = [sb.tile([P, HALF], F32, name="ts_listed%d" % h, align_bytes=64) for h in range(2)]
-        nc.vector.tensor_copy(ts_listed[1][:], ts_pool[:].indirect(halves[1]))
-        scales_listed = [
-            shared.tile([P, HALF // 4], I32, name="scales_listed%d" % h, align_bytes=64, offset=(1024, 0)[h])
-            for h in range(2)
-        ]
-        nc.vector.tensor_copy(scales_listed[0][:].bitcast(U8), scale_pool[:].bitcast(U8).indirect(halves[0]))
+        scales_listed = sb.tile([P, SLOTS // 4], I32, name="scales_listed", align_bytes=64)
+        nc.vector.tensor_copy(scales_listed[:].bitcast(U8), scale_pool[:].bitcast(U8).indirect(offsets[:]))
+        for quad in range(4):
+            nc.sync.dma_start(
+                planes[32 * quad : 32 * quad + 4, :],
+                scales_listed[SCALE_ROW + 4 * quad : SCALE_ROW + 4 * quad + 4, :],
+            )
+        key_scales = planes[:].bitcast(U8)
 
-        q_grouped = shared.tile([P, QUERIES, PACK], BF16, name="q_grouped", align_bytes=64, offset=0)
+        q_grouped = shared.tile([P, QUERIES, PACK], BF16, name="q_grouped", align_bytes=64, offset=POOL)
         nc.scalar.copy(q_grouped[:], q_raw[:].rearrange("p j w -> p w j"))
-        q_words = sb.tile([P, QUERIES], U32, name="q_words", align_bytes=64)
-        q_scales = planes[:, SLOTS // 4 :].bitcast(U8)
+        q_words = shared.tile([P, QUERIES], U32, name="q_words", align_bytes=64, offset=0)
+        q_scales = sb.tile([P, QUERIES], U8, name="q_scales", align_bytes=64)
         nc.vector.quantize_mx(
-            out=q_words[:].bitcast(FP8X4), scales=q_scales, in_=q_grouped[:].rearrange("p w j -> p (w j)")
+            out=q_words[:].bitcast(FP8X4), scales=q_scales[:], in_=q_grouped[:].rearrange("p w j -> p (w j)")
         )
 
-        scales_dealt = sb.tile([P, HALF // 4], I32, name="scales_dealt", align_bytes=64)
-        nc.vector.tensor_copy(
-            scales_dealt[:].rearrange("p (k j w) -> p k j w", k=2, j=4),
-            scales_listed[0][:].rearrange("p (j k w) -> p k j w", k=2, j=4),
-        )
-        nc.vector.tensor_copy(scales_listed[1][:].bitcast(U8), scale_pool[:].bitcast(U8).indirect(halves[1]))
-        nc.vector.tensor_copy(ts_listed[0][:], ts_pool[:].indirect(halves[0]))
+        per = PIECE // SEG
+        ts_listed = []
+        for k in range(PIECES):
+            t = sb.tile([P, PIECE], F32, name="ts_listed%d" % k, align_bytes=64)
+            nc.scalar.activation(t[:], ts_pool[:].indirect(pieces[k]), COPY)
+            ts_listed.append(t)
+        ts_cols = []
+        for k in range(PIECES):
+            turned = ps.tile([P, per, SEG], F32, name="turned%d" % k, tag="bank%d" % (4 + k))
+            for j in range(per):
+                nc.tensor.transpose(turned[:, j, :], ts_listed[k][:, j * SEG : (j + 1) * SEG], identity[:])
+            c = sb.tile([P, per], F32, name="ts_cols%d" % k, align_bytes=64)
+            nc.scalar.copy(c[:], turned[:, :, TS_ROW])
+            ts_cols.append(c)
+        ts_spread = []
+        for k in range(PIECES):
+            spread = ps.tile([P, per, SEG], F32, name="spread%d" % k, tag="bank%d" % k)
+            for j in range(per):
+                nc.tensor.transpose(spread[:, j, :], ts_cols[k][:, j : j + 1].to_broadcast([P, P]), identity[:])
+            s = sb.tile([P, PIECE], F32, name="ts_spread%d" % k, align_bytes=64)
+            nc.scalar.copy(s[:], spread[:].rearrange("p j s -> p (j s)"))
+            ts_spread.append(s)
 
-        turned1 = ps.tile([P, 4, SEG], F32, name="turned1", tag="bank0")
-        for j in range(4):
-            nc.tensor.transpose(turned1[:, j, :], ts_listed[1][:, j * SEG : (j + 1) * SEG], identity[:])
-        ts_cols1 = sb.tile([P, 4], F32, name="ts_cols1", align_bytes=64)
-        nc.scalar.copy(ts_cols1[:], turned1[:, :, TS_ROW])
-        spread = ps.tile([P, 4, SEG], F32, name="spread", tag="bank1")
-        for j in range(4):
-            nc.tensor.transpose(spread[:, j, :], ts_cols1[:, j : j + 1].to_broadcast([P, P]), identity[:])
-        ts_spread = sb.tile([P, HALF], F32, name="ts_spread", align_bytes=64)
-        nc.scalar.copy(ts_spread[:], spread[:].rearrange("p j s -> p (j s)"))
-        ts_dealt = sb.tile([P, HALF], F32, name="ts_dealt", align_bytes=64)
-        nc.scalar.copy(
-            ts_dealt[:].rearrange("p (k j s) -> p k j s", k=2, j=4),
-            ts_listed[0][:].rearrange("p (j k s) -> p k j s", k=2, j=4),
-        )
-        turned0 = ps.tile([P, 4, SEG], F32, name="turned0", tag="bank2")
-        for j in range(4):
-            nc.tensor.transpose(turned0[:, j, :], ts_dealt[:, j * SEG : (j + 1) * SEG], identity[:])
-        ts_cols0 = sb.tile([P, 4], F32, name="ts_cols0", align_bytes=64)
-        nc.scalar.copy(ts_cols0[:], turned0[:, :, TS_ROW])
-
-        for h, moved in enumerate((scales_dealt, scales_listed[1])):
-            for quad in range(4):
-                nc.sync.dma_start(
-                    planes[32 * quad : 32 * quad + 4, h * HALF // 4 : (h + 1) * HALF // 4],
-                    moved[SCALE_ROW + 4 * quad : SCALE_ROW + 4 * quad + 4, :],
-                )
-        key_scales = planes[:, 0 : SLOTS // 4].bitcast(U8)
-
-        key_words = shared.tile([P, SLOTS], U32, name="key_words", align_bytes=64, offset=512)
-        nc.vector.tensor_copy(
-            key_words[:, 0:HALF].rearrange("p (k j s) -> p j k s", k=2, j=4),
-            word_pool[:].bitcast(U32).indirect(halves[0]),
-        )
-        nc.vector.tensor_copy(key_words[:, HALF:SLOTS], word_pool[:].bitcast(U32).indirect(halves[1]))
-
-        def by_slot(acc, t):
-            nc.tensor.matmul_mx(
-                out=acc,
-                lhsT=key_words[:, t * SEG : (t + 1) * SEG].bitcast(FP8X4),
-                lhsT_scale=key_scales[:, t * SEG : (t + 1) * SEG],
-                rhs=q_words[:].bitcast(FP8X4),
-                rhs_scale=q_scales,
-                start=True,
-                stop=True,
+        key_words = shared.tile([P, SLOTS], U32, name="key_words", align_bytes=64, offset=POOL)
+        for k in range(PIECES):
+            nc.vector.tensor_copy(
+                key_words[:, k * PIECE : (k + 1) * PIECE], word_pool[:].bitcast(U32).indirect(pieces[k])
             )
 
-        lower = []
-        for a in range(2):
-            acc = ps.tile([P, QUERIES], F32, name="lower%d" % a, tag="bank%d" % a)
-            by_slot(acc[:], a)
-            y = sb.tile([P, QUERIES], F32, name="lower_scaled%d" % a, align_bytes=64)
-            nc.scalar.activation(y[:], acc[:], COPY, scale=ts_cols0[:, a : a + 1])
-            lower.append(y)
-        upper = ps.tile([P, 2, QUERIES], F32, name="upper", tag="bank2")
-        for a in range(2):
-            by_slot(upper[:, a, :], 2 + a)
-
-        widths = (SEG, SEG, 2 * SEG)
-        scores = []
-        at = HALF
-        for c, width in enumerate(widths):
-            acc = ps.tile([P, width], F32, name="scores%d" % c)
+        scaled = []
+        for k in range(PIECES):
+            acc = ps.tile([P, PIECE], F32, name="scores%d" % k, tag="bank%d" % k)
             nc.tensor.matmul_mx(
                 out=acc[:],
                 lhsT=q_words[:].bitcast(FP8X4),
-                lhsT_scale=q_scales,
-                rhs=key_words[:, at : at + width].bitcast(FP8X4),
-                rhs_scale=key_scales[:, at : at + width],
+                lhsT_scale=q_scales[:],
+                rhs=key_words[:, k * PIECE : (k + 1) * PIECE].bitcast(FP8X4),
+                rhs_scale=key_scales[:, k * PIECE : (k + 1) * PIECE],
                 start=True,
                 stop=True,
             )
-            scores.append(acc)
-            at = at + width
-
-        folded = []
-        for a in range(2):
-            z = sb.tile([P, QUERIES], F32, name="folded%d" % a, align_bytes=64)
-            nc.vector.scalar_tensor_tensor(z[:], upper[:, a, :], ts_cols0[:, 2 + a : 3 + a], lower[a][:], MULT, MAX)
-            folded.append(z)
-        back = ps.tile([P, 2, P], F32, name="back")
-        for a in range(2):
-            nc.tensor.transpose(back[:, a, :], folded[a][:], identity[:])
+            y = sb.tile([P, PIECE], F32, name="scaled%d" % k, align_bytes=64)
+            nc.vector.tensor_tensor(y[:], acc[:], ts_spread[k][:], MULT)
+            scaled.append(y)
 
         best = sb.tile([P, PASSAGES], F32, name="best", align_bytes=64)
-        scaled = [sb.tile([P, CHUNK], F32, name="scaled%d" % c, align_bytes=64) for c in range(2)]
-        nc.vector.tensor_tensor(scaled[0][:, 0:SEG], scores[0][:], ts_spread[:, 0:SEG], MULT)
-        nc.vector.tensor_tensor(scaled[0][:, SEG:CHUNK], scores[1][:], ts_spread[:, SEG:CHUNK], MULT)
-        nc.vector.tensor_tensor(scaled[1][:], scores[2][:], ts_spread[:, CHUNK:HALF], MULT)
-        nc.vector.tensor_reduce(best[:, 4:6], scaled[0][:].rearrange("p (j s) -> p j s", s=SEG), AXIS_X, MAX)
-        nc.vector.tensor_reduce(best[:, 6:8], scaled[1][:].rearrange("p (j s) -> p j s", s=SEG), AXIS_X, MAX)
-        nc.vector.tensor_reduce(best[:, 0:4], back[:].rearrange("p a (j s) -> p (a j) s", j=2), AXIS_X, MAX)
+        for k in range(PIECES):
+            nc.vector.tensor_reduce(
+                best[:, k * per : (k + 1) * per], scaled[k][:].rearrange("p (j s) -> p j s", s=SEG), AXIS_X, MAX
+            )
         nc.sync.dma_start(out[0], best[:])

@@ -23,6 +23,7 @@ QUERIES = 128
 SEG = 128
 PASSAGES = SLOTS // SEG
 LIST_COLS = SLOTS // 16
+HALF = SLOTS // 2
 PIECES = 4
 PIECE = SLOTS // PIECES
 TS_ROW = P - 1
@@ -43,94 +44,101 @@ def tile_attend_maxsim_ts_kernel(tc, qT, k_words, k_scales, ts, offs, out):
         ts_pool = sb.tile([P, POOL], F32, name="ts_pool", align_bytes=64)
         q_raw = sb.tile([P, PACK, QUERIES], F32, name="q_raw", align_bytes=64)
         word_pool = sb.tile([P, POOL], I32, name="word_pool", align_bytes=64)
-        scale_pool = shared.tile([P, POOL // 4], I32, name="scale_pool", align_bytes=64, offset=0)
-        planes = sb.tile([P, SLOTS // 4], I32, name="planes", align_bytes=64)
+        scale_pool = shared.tile([P, POOL // 4], I32, name="scale_pool", align_bytes=64, offset=1024)
+        planes = sb.tile([P, (SLOTS + QUERIES) // 4], I32, name="planes", align_bytes=64)
         identity = sb.tile([P, P], F32, name="identity", align_bytes=64)
 
-        nc.sync.dma_start(offsets[:], offs)
         nc.sync.dma_start(ts_pool[TS_ROW:P, :], ts[0:1, :])
+        nc.sync.dma_start(offsets[:], offs)
         nc.scalar.dma_start(q_raw[:], qT[0].rearrange("(p j) w -> p j w", j=PACK))
         nc.scalar.dma_start(scale_pool[SCALE_ROW:P, :], k_scales[0].bitcast(I32))
         nc.scalar.dma_start(word_pool[:], k_words[0].rearrange("p n t -> p (n t)").bitcast(I32))
 
+        nc.vector.memset(ts_pool[0:TS_ROW, 0:611], 0.0)
+        nc.vector.memset(ts_pool[0:TS_ROW, 611:1224], 0.0)
+        nc.gpsimd.memset(ts_pool[0:TS_ROW, 1224:POOL], 0.0)
+        nc.gpsimd.memset(scale_pool[0:SCALE_ROW, :], 0)
         make_identity(nc, identity[:])
-        nc.vector.memset(ts_pool[0:TS_ROW, 0:1151], 0.0)
-        nc.vector.memset(ts_pool[0:TS_ROW, 1151:2304], 0.0)
-        nc.gpsimd.memset(ts_pool[0:TS_ROW, 2304:2560], 0.0)
-        nc.gpsimd.memset(ts_pool[0:TS_ROW, 2560:POOL], 0.0)
-        nc.vector.memset(scale_pool[0:SCALE_ROW, 0:255], 0)
-        nc.vector.memset(scale_pool[0:SCALE_ROW, 255:512], 0)
-        nc.gpsimd.memset(scale_pool[0:SCALE_ROW, 512 : POOL // 4], 0)
         nc.gpsimd.memset(planes[:], 0)
 
         cols = LIST_COLS // PIECES
         pieces = [offsets[:, k * cols : (k + 1) * cols] for k in range(PIECES)]
+        halves = [offsets[:, h * LIST_COLS // 2 : (h + 1) * LIST_COLS // 2] for h in range(2)]
 
-        scales_listed = sb.tile([P, SLOTS // 4], I32, name="scales_listed", align_bytes=64)
-        nc.vector.tensor_copy(scales_listed[:].bitcast(U8), scale_pool[:].bitcast(U8).indirect(offsets[:]))
-        for quad in range(4):
-            nc.sync.dma_start(
-                planes[32 * quad : 32 * quad + 4, :],
-                scales_listed[SCALE_ROW + 4 * quad : SCALE_ROW + 4 * quad + 4, :],
-            )
-        key_scales = planes[:].bitcast(U8)
+        ts_listed = [sb.tile([P, HALF], F32, name="ts_listed%d" % h, align_bytes=64) for h in range(2)]
+        for h in range(2):
+            nc.vector.tensor_copy(ts_listed[h][:], ts_pool[:].indirect(halves[h]))
 
-        q_grouped = shared.tile([P, QUERIES, PACK], BF16, name="q_grouped", align_bytes=64, offset=POOL)
+        scales_first = sb.tile([P, HALF // 4], I32, name="scales_first", align_bytes=64)
+        nc.vector.tensor_copy(scales_first[:].bitcast(U8), scale_pool[:].bitcast(U8).indirect(halves[0]))
+
+        scales_second = sb.tile([P, HALF // 4], I32, name="scales_second", align_bytes=64)
+        nc.vector.tensor_copy(scales_second[:].bitcast(U8), scale_pool[:].bitcast(U8).indirect(halves[1]))
+
+        q_grouped = shared.tile([P, QUERIES, PACK], BF16, name="q_grouped", align_bytes=64, offset=0)
         nc.scalar.copy(q_grouped[:], q_raw[:].rearrange("p j w -> p w j"))
-        q_words = shared.tile([P, QUERIES], U32, name="q_words", align_bytes=64, offset=0)
-        q_scales = sb.tile([P, QUERIES], U8, name="q_scales", align_bytes=64)
+        q_words = shared.tile([P, QUERIES], U32, name="q_words", align_bytes=64, offset=POOL)
+        q_scales = planes[:, SLOTS // 4 :].bitcast(U8)
         nc.vector.quantize_mx(
-            out=q_words[:].bitcast(FP8X4), scales=q_scales[:], in_=q_grouped[:].rearrange("p w j -> p (w j)")
+            out=q_words[:].bitcast(FP8X4), scales=q_scales, in_=q_grouped[:].rearrange("p w j -> p (w j)")
         )
 
+        for h, moved in enumerate((scales_first, scales_second)):
+            for quad in range(4):
+                nc.sync.dma_start(
+                    planes[32 * quad : 32 * quad + 4, h * HALF // 4 : (h + 1) * HALF // 4],
+                    moved[SCALE_ROW + 4 * quad : SCALE_ROW + 4 * quad + 4, :],
+                )
+        key_scales = planes[:, 0 : SLOTS // 4].bitcast(U8)
+
         per = PIECE // SEG
-        ts_listed = []
-        for k in range(PIECES):
-            t = sb.tile([P, PIECE], F32, name="ts_listed%d" % k, align_bytes=64)
-            nc.scalar.activation(t[:], ts_pool[:].indirect(pieces[k]), COPY)
-            ts_listed.append(t)
         ts_cols = []
-        for k in range(PIECES):
-            turned = ps.tile([P, per, SEG], F32, name="turned%d" % k, tag="bank%d" % (4 + k))
-            for j in range(per):
-                nc.tensor.transpose(turned[:, j, :], ts_listed[k][:, j * SEG : (j + 1) * SEG], identity[:])
-            c = sb.tile([P, per], F32, name="ts_cols%d" % k, align_bytes=64)
+        for h in range(2):
+            turned = ps.tile([P, 4, SEG], F32, name="turned%d" % h, tag="bank%d" % (4 + h))
+            for j in range(4):
+                nc.tensor.transpose(turned[:, j, :], ts_listed[h][:, j * SEG : (j + 1) * SEG], identity[:])
+            c = sb.tile([P, 4], F32, name="ts_cols%d" % h, align_bytes=64)
             nc.scalar.copy(c[:], turned[:, :, TS_ROW])
             ts_cols.append(c)
         ts_spread = []
-        for k in range(PIECES):
-            spread = ps.tile([P, per, SEG], F32, name="spread%d" % k, tag="bank%d" % k)
-            for j in range(per):
-                nc.tensor.transpose(spread[:, j, :], ts_cols[k][:, j : j + 1].to_broadcast([P, P]), identity[:])
-            s = sb.tile([P, PIECE], F32, name="ts_spread%d" % k, align_bytes=64)
+        for h in range(2):
+            spread = ps.tile([P, 4, SEG], F32, name="spread%d" % h, tag="bank%d" % (6 + h))
+            for j in range(4):
+                nc.tensor.transpose(spread[:, j, :], ts_cols[h][:, j : j + 1].to_broadcast([P, P]), identity[:])
+            s = sb.tile([P, HALF], F32, name="ts_spread%d" % h, align_bytes=64)
             nc.scalar.copy(s[:], spread[:].rearrange("p j s -> p (j s)"))
-            ts_spread.append(s)
+            ts_spread.extend([s[:, 0:PIECE], s[:, PIECE:HALF]])
 
-        key_words = shared.tile([P, SLOTS], U32, name="key_words", align_bytes=64, offset=POOL)
+        key_words = shared.tile([P, SLOTS], U32, name="key_words", align_bytes=64, offset=0)
         for k in range(PIECES):
             nc.vector.tensor_copy(
                 key_words[:, k * PIECE : (k + 1) * PIECE], word_pool[:].bitcast(U32).indirect(pieces[k])
             )
 
-        scaled = []
+        scores = []
         for k in range(PIECES):
             acc = ps.tile([P, PIECE], F32, name="scores%d" % k, tag="bank%d" % k)
             nc.tensor.matmul_mx(
                 out=acc[:],
                 lhsT=q_words[:].bitcast(FP8X4),
-                lhsT_scale=q_scales[:],
+                lhsT_scale=q_scales,
                 rhs=key_words[:, k * PIECE : (k + 1) * PIECE].bitcast(FP8X4),
                 rhs_scale=key_scales[:, k * PIECE : (k + 1) * PIECE],
                 start=True,
                 stop=True,
             )
-            y = sb.tile([P, PIECE], F32, name="scaled%d" % k, align_bytes=64)
-            nc.vector.tensor_tensor(y[:], acc[:], ts_spread[k][:], MULT)
-            scaled.append(y)
+            scores.append(acc)
 
         best = sb.tile([P, PASSAGES], F32, name="best", align_bytes=64)
-        for k in range(PIECES):
-            nc.vector.tensor_reduce(
-                best[:, k * per : (k + 1) * per], scaled[k][:].rearrange("p (j s) -> p j s", s=SEG), AXIS_X, MAX
-            )
+        scaled = [sb.tile([P, PIECE], F32, name="scaled%d" % k, align_bytes=64) for k in range(PIECES)]
+        for k in range(PIECES + 1):
+            if k < PIECES:
+                nc.vector.tensor_tensor(scaled[k][:], scores[k][:], ts_spread[k], MULT)
+            if k > 0:
+                nc.vector.tensor_reduce(
+                    best[:, (k - 1) * per : k * per],
+                    scaled[k - 1][:].rearrange("p (j s) -> p j s", s=SEG),
+                    AXIS_X,
+                    MAX,
+                )
         nc.sync.dma_start(out[0], best[:])

@@ -24,8 +24,8 @@ SEG = 128
 PASSAGES = SLOTS // SEG
 LIST_COLS = SLOTS // 16
 HALF = SLOTS // 2
-PIECES = 4
-PIECE = SLOTS // PIECES
+PIECES = (3, 3, 2)
+TURNED = (2, 4)
 TS_ROW = P - 1
 SCALE_ROW = P - 16
 
@@ -54,26 +54,25 @@ def tile_attend_maxsim_ts_kernel(tc, qT, k_words, k_scales, ts, offs, out):
         nc.scalar.dma_start(scale_pool[SCALE_ROW:P, :], k_scales[0].bitcast(I32))
         nc.scalar.dma_start(word_pool[:], k_words[0].rearrange("p n t -> p (n t)").bitcast(I32))
 
-        nc.vector.memset(ts_pool[0:TS_ROW, 0:611], 0.0)
-        nc.vector.memset(ts_pool[0:TS_ROW, 611:1224], 0.0)
-        nc.gpsimd.memset(ts_pool[0:TS_ROW, 1224:POOL], 0.0)
+        nc.vector.memset(ts_pool[0:TS_ROW, 0:671], 0.0)
+        nc.vector.memset(ts_pool[0:TS_ROW, 671:1344], 0.0)
+        nc.gpsimd.memset(ts_pool[0:TS_ROW, 1344:POOL], 0.0)
         nc.gpsimd.memset(scale_pool[0:SCALE_ROW, :], 0)
         make_identity(nc, identity[:])
         nc.gpsimd.memset(planes[:], 0)
 
-        cols = LIST_COLS // PIECES
-        pieces = [offsets[:, k * cols : (k + 1) * cols] for k in range(PIECES)]
         halves = [offsets[:, h * LIST_COLS // 2 : (h + 1) * LIST_COLS // 2] for h in range(2)]
 
         ts_listed = [sb.tile([P, HALF], F32, name="ts_listed%d" % h, align_bytes=64) for h in range(2)]
         for h in range(2):
             nc.vector.tensor_copy(ts_listed[h][:], ts_pool[:].indirect(halves[h]))
 
-        scales_first = sb.tile([P, HALF // 4], I32, name="scales_first", align_bytes=64)
-        nc.vector.tensor_copy(scales_first[:].bitcast(U8), scale_pool[:].bitcast(U8).indirect(halves[0]))
-
-        scales_second = sb.tile([P, HALF // 4], I32, name="scales_second", align_bytes=64)
-        nc.vector.tensor_copy(scales_second[:].bitcast(U8), scale_pool[:].bitcast(U8).indirect(halves[1]))
+        scales_listed = sb.tile([P, SLOTS // 4], I32, name="scales_listed", align_bytes=64)
+        for h in range(2):
+            nc.vector.tensor_copy(
+                scales_listed[:, h * HALF // 4 : (h + 1) * HALF // 4].bitcast(U8),
+                scale_pool[:].bitcast(U8).indirect(halves[h]),
+            )
 
         q_grouped = shared.tile([P, QUERIES, PACK], BF16, name="q_grouped", align_bytes=64, offset=0)
         nc.scalar.copy(q_grouped[:], q_raw[:].rearrange("p j w -> p w j"))
@@ -83,62 +82,96 @@ def tile_attend_maxsim_ts_kernel(tc, qT, k_words, k_scales, ts, offs, out):
             out=q_words[:].bitcast(FP8X4), scales=q_scales, in_=q_grouped[:].rearrange("p w j -> p (w j)")
         )
 
-        for h, moved in enumerate((scales_first, scales_second)):
-            for quad in range(4):
-                nc.sync.dma_start(
-                    planes[32 * quad : 32 * quad + 4, h * HALF // 4 : (h + 1) * HALF // 4],
-                    moved[SCALE_ROW + 4 * quad : SCALE_ROW + 4 * quad + 4, :],
-                )
+        first, second, both = slice(0, HALF // 4), slice(HALF // 4, SLOTS // 4), slice(0, SLOTS // 4)
+        for quad, at in [(q, first) for q in range(3)] + [(3, both)] + [(q, second) for q in range(3)]:
+            nc.sync.dma_start(
+                planes[32 * quad : 32 * quad + 4, at],
+                scales_listed[SCALE_ROW + 4 * quad : SCALE_ROW + 4 * quad + 4, at],
+            )
         key_scales = planes[:, 0 : SLOTS // 4].bitcast(U8)
 
-        per = PIECE // SEG
         ts_cols = []
         for h in range(2):
-            turned = ps.tile([P, 4, SEG], F32, name="turned%d" % h, tag="bank%d" % (4 + h))
+            turned = ps.tile([P, 4, SEG], F32, name="turned%d" % h, tag="bank%d" % (5 + h))
             for j in range(4):
                 nc.tensor.transpose(turned[:, j, :], ts_listed[h][:, j * SEG : (j + 1) * SEG], identity[:])
             c = sb.tile([P, 4], F32, name="ts_cols%d" % h, align_bytes=64)
             nc.scalar.copy(c[:], turned[:, :, TS_ROW])
-            ts_cols.append(c)
-        ts_spread = []
+            ts_cols.extend([c[:, j : j + 1] for j in range(4)])
+        ts_spread = {}
         for h in range(2):
-            spread = ps.tile([P, 4, SEG], F32, name="spread%d" % h, tag="bank%d" % (6 + h))
-            for j in range(4):
-                nc.tensor.transpose(spread[:, j, :], ts_cols[h][:, j : j + 1].to_broadcast([P, P]), identity[:])
-            s = sb.tile([P, HALF], F32, name="ts_spread%d" % h, align_bytes=64)
+            direct = [j for j in range(4 * h, 4 * h + 4) if j not in TURNED]
+            spread = ps.tile([P, 3, SEG], F32, name="spread%d" % h, tag="bank%d" % (4, 7)[h])
+            for i, j in enumerate(direct):
+                nc.tensor.transpose(spread[:, i, :], ts_cols[j].to_broadcast([P, P]), identity[:])
+            s = sb.tile([P, 3 * SEG], F32, name="ts_spread%d" % h, align_bytes=64)
             nc.scalar.copy(s[:], spread[:].rearrange("p j s -> p (j s)"))
-            ts_spread.extend([s[:, 0:PIECE], s[:, PIECE:HALF]])
+            for i, j in enumerate(direct):
+                ts_spread.setdefault(j, (s, i * SEG))
 
         key_words = shared.tile([P, SLOTS], U32, name="key_words", align_bytes=64, offset=0)
-        for k in range(PIECES):
+        at = 0
+        for count in PIECES:
             nc.vector.tensor_copy(
-                key_words[:, k * PIECE : (k + 1) * PIECE], word_pool[:].bitcast(U32).indirect(pieces[k])
+                key_words[:, at * SEG : (at + count) * SEG],
+                word_pool[:].bitcast(U32).indirect(offsets[:, at * SEG // 16 : (at + count) * SEG // 16]),
             )
+            at = at + count
 
-        scores = []
-        for k in range(PIECES):
-            acc = ps.tile([P, PIECE], F32, name="scores%d" % k, tag="bank%d" % k)
+        def score(acc, stationary, stationary_scale, moving, moving_scale):
             nc.tensor.matmul_mx(
-                out=acc[:],
-                lhsT=q_words[:].bitcast(FP8X4),
-                lhsT_scale=q_scales,
-                rhs=key_words[:, k * PIECE : (k + 1) * PIECE].bitcast(FP8X4),
-                rhs_scale=key_scales[:, k * PIECE : (k + 1) * PIECE],
+                out=acc,
+                lhsT=stationary.bitcast(FP8X4),
+                lhsT_scale=stationary_scale,
+                rhs=moving.bitcast(FP8X4),
+                rhs_scale=moving_scale,
                 start=True,
                 stop=True,
             )
-            scores.append(acc)
+
+        scores = {}
+        by_slot = {}
+        for j, count in ((0, 1), (1, 1), (2, 1), (3, 1), (4, 1), (5, 1), (6, 2)):
+            at = slice(j * SEG, (j + count) * SEG)
+            acc = ps.tile([P, count * SEG], F32, name="scores%d" % j, tag="bank%d" % j)
+            if j in TURNED:
+                score(acc[:], key_words[:, at], key_scales[:, at], q_words[:], q_scales)
+                y = sb.tile([P, QUERIES], F32, name="slot_scaled%d" % j, align_bytes=64)
+                nc.scalar.activation(y[:], acc[:], COPY, scale=ts_cols[j])
+                by_slot.setdefault(j, y)
+            else:
+                score(acc[:], q_words[:], q_scales, key_words[:, at], key_scales[:, at])
+                scores.setdefault(j, acc)
+        back = {}
+        for j in TURNED:
+            t = ps.tile([P, SEG], F32, name="back%d" % j, tag="bank%d" % j)
+            nc.tensor.transpose(t[:], by_slot[j][:], identity[:])
+            back.setdefault(j, t)
 
         best = sb.tile([P, PASSAGES], F32, name="best", align_bytes=64)
-        scaled = [sb.tile([P, PIECE], F32, name="scaled%d" % k, align_bytes=64) for k in range(PIECES)]
-        for k in range(PIECES + 1):
-            if k < PIECES:
-                nc.vector.tensor_tensor(scaled[k][:], scores[k][:], ts_spread[k], MULT)
-            if k > 0:
-                nc.vector.tensor_reduce(
-                    best[:, (k - 1) * per : k * per],
-                    scaled[k - 1][:].rearrange("p (j s) -> p j s", s=SEG),
-                    AXIS_X,
-                    MAX,
-                )
+        scaled = {}
+
+        def product(j, count):
+            y = sb.tile([P, count * SEG], F32, name="scaled%d" % j, align_bytes=64)
+            s, at = ts_spread[j]
+            nc.vector.tensor_tensor(y[:], scores[j][:], s[:, at : at + count * SEG], MULT)
+            scaled.setdefault(j, y)
+
+        def maximum(j, count, source):
+            nc.vector.tensor_reduce(
+                best[:, j : j + count], source[:].rearrange("p (j s) -> p j s", s=SEG), AXIS_X, MAX
+            )
+
+        product(0, 1)
+        product(1, 1)
+        maximum(0, 1, scaled[0])
+        product(3, 1)
+        maximum(1, 1, scaled[1])
+        product(5, 1)
+        maximum(3, 1, scaled[3])
+        product(6, 2)
+        maximum(5, 1, scaled[5])
+        maximum(2, 1, back[2])
+        maximum(6, 2, scaled[6])
+        maximum(4, 1, back[4])
         nc.sync.dma_start(out[0], best[:])

@@ -27,7 +27,9 @@ HALF = SLOTS // 2
 PIECES = (3, 3, 2)
 TURNED = (2, 4)
 TS_ROW = P - 1
-SCALE_ROW = P - 16
+SCALE_ROW = 32
+SCALE_ZERO_SPLIT = 576
+TS_ZERO_SPLIT = 2192
 
 FLOPS = 2 * QUERIES * SLOTS * P * PACK
 BYTES = P * POOL * 4 + 16 * POOL + P * PACK * QUERIES * 4 + POOL * 4 + P * LIST_COLS * 2 + QUERIES * PASSAGES * 4
@@ -48,24 +50,26 @@ def tile_attend_maxsim_ts_kernel(tc, qT, k_words, k_scales, ts, offs, out):
         planes = sb.tile([P, (SLOTS + QUERIES) // 4], I32, name="planes", align_bytes=64)
         identity = sb.tile([P, P], F32, name="identity", align_bytes=64)
 
+        nc.vector.memset(scale_pool[:, 0 : SCALE_ZERO_SPLIT // 2 - 1], 0)
+        nc.vector.memset(scale_pool[:, SCALE_ZERO_SPLIT // 2 - 1 : SCALE_ZERO_SPLIT], 0)
+        nc.gpsimd.memset(scale_pool[:, SCALE_ZERO_SPLIT:], 0)
+
         nc.sync.dma_start(ts_pool[TS_ROW:P, :], ts[0:1, :])
         nc.sync.dma_start(offsets[:], offs)
         nc.scalar.dma_start(q_raw[:], qT[0].rearrange("(p j) w -> p j w", j=PACK))
-        nc.scalar.dma_start(scale_pool[SCALE_ROW:P, :], k_scales[0].bitcast(I32))
         nc.scalar.dma_start(word_pool[:], k_words[0].rearrange("p n t -> p (n t)").bitcast(I32))
+        nc.sync.dma_start(scale_pool[SCALE_ROW : SCALE_ROW + 64 : 4, :], k_scales[0].bitcast(I32))
 
-        nc.vector.memset(ts_pool[0:TS_ROW, 0:671], 0.0)
-        nc.vector.memset(ts_pool[0:TS_ROW, 671:1344], 0.0)
-        nc.gpsimd.memset(ts_pool[0:TS_ROW, 1344:POOL], 0.0)
-        nc.gpsimd.memset(scale_pool[0:SCALE_ROW, :], 0)
+        nc.vector.memset(ts_pool[0:TS_ROW, 0 : TS_ZERO_SPLIT // 2 - 1], 0.0)
+        nc.vector.memset(ts_pool[0:TS_ROW, TS_ZERO_SPLIT // 2 - 1 : TS_ZERO_SPLIT], 0.0)
+        nc.gpsimd.memset(ts_pool[0:TS_ROW, TS_ZERO_SPLIT:POOL], 0.0)
         make_identity(nc, identity[:])
         nc.gpsimd.memset(planes[:], 0)
 
         halves = [offsets[:, h * LIST_COLS // 2 : (h + 1) * LIST_COLS // 2] for h in range(2)]
 
-        ts_listed = [sb.tile([P, HALF], F32, name="ts_listed%d" % h, align_bytes=64) for h in range(2)]
-        for h in range(2):
-            nc.vector.tensor_copy(ts_listed[h][:], ts_pool[:].indirect(halves[h]))
+        ts_first = sb.tile([P, HALF], F32, name="ts_first", align_bytes=64)
+        nc.vector.tensor_copy(ts_first[:], ts_pool[:].indirect(halves[0]))
 
         scales_listed = sb.tile([P, SLOTS // 4], I32, name="scales_listed", align_bytes=64)
         for h in range(2):
@@ -73,6 +77,10 @@ def tile_attend_maxsim_ts_kernel(tc, qT, k_words, k_scales, ts, offs, out):
                 scales_listed[:, h * HALF // 4 : (h + 1) * HALF // 4].bitcast(U8),
                 scale_pool[:].bitcast(U8).indirect(halves[h]),
             )
+
+        ts_second = shared.tile([P, HALF], F32, name="ts_second", align_bytes=64, offset=POOL + 4 * QUERIES)
+        nc.vector.tensor_copy(ts_second[:], ts_pool[:].indirect(halves[1]))
+        ts_listed = [ts_first, ts_second]
 
         q_grouped = shared.tile([P, QUERIES, PACK], BF16, name="q_grouped", align_bytes=64, offset=0)
         nc.scalar.copy(q_grouped[:], q_raw[:].rearrange("p j w -> p w j"))
@@ -83,10 +91,11 @@ def tile_attend_maxsim_ts_kernel(tc, qT, k_words, k_scales, ts, offs, out):
         )
 
         first, second, both = slice(0, HALF // 4), slice(HALF // 4, SLOTS // 4), slice(0, SLOTS // 4)
-        for quad, at in [(q, first) for q in range(3)] + [(3, both)] + [(q, second) for q in range(3)]:
+        for quad, at in [(0, first), (1, first), (2, both), (3, both), (0, second), (1, second)]:
             nc.sync.dma_start(
                 planes[32 * quad : 32 * quad + 4, at],
-                scales_listed[SCALE_ROW + 4 * quad : SCALE_ROW + 4 * quad + 4, at],
+                scales_listed[SCALE_ROW + 16 * quad : SCALE_ROW + 16 * quad + 16 : 4, at],
+                max_dma_last_dim=512,
             )
         key_scales = planes[:, 0 : SLOTS // 4].bitcast(U8)
 

@@ -28,8 +28,8 @@ PIECES = (3, 3, 2)
 TURNED = (2, 4)
 TS_ROW = P - 1
 SCALE_ROW = 32
-SCALE_ZERO_SPLIT = 576
-TS_ZERO_SPLIT = 2192
+SCALE_ZERO_SPLIT = 416
+TS_ZERO_SPLIT = 2016
 
 FLOPS = 2 * QUERIES * SLOTS * P * PACK
 BYTES = P * POOL * 4 + 16 * POOL + P * PACK * QUERIES * 4 + POOL * 4 + P * LIST_COLS * 2 + QUERIES * PASSAGES * 4
@@ -54,11 +54,11 @@ def tile_attend_maxsim_ts_kernel(tc, qT, k_words, k_scales, ts, offs, out):
         nc.vector.memset(scale_pool[:, SCALE_ZERO_SPLIT // 2 - 1 : SCALE_ZERO_SPLIT], 0)
         nc.gpsimd.memset(scale_pool[:, SCALE_ZERO_SPLIT:], 0)
 
-        nc.sync.dma_start(ts_pool[TS_ROW:P, :], ts[0:1, :])
+        nc.scalar.dma_start(ts_pool[TS_ROW:P, :], ts[0:1, :])
+        nc.sync.dma_start(q_raw[:], qT[0].rearrange("(p j) w -> p j w", j=PACK))
         nc.sync.dma_start(offsets[:], offs)
-        nc.scalar.dma_start(q_raw[:], qT[0].rearrange("(p j) w -> p j w", j=PACK))
+        nc.scalar.dma_start(scale_pool[SCALE_ROW : SCALE_ROW + 64 : 4, :], k_scales[0].bitcast(I32))
         nc.scalar.dma_start(word_pool[:], k_words[0].rearrange("p n t -> p (n t)").bitcast(I32))
-        nc.sync.dma_start(scale_pool[SCALE_ROW : SCALE_ROW + 64 : 4, :], k_scales[0].bitcast(I32))
 
         nc.vector.memset(ts_pool[0:TS_ROW, 0 : TS_ZERO_SPLIT // 2 - 1], 0.0)
         nc.vector.memset(ts_pool[0:TS_ROW, TS_ZERO_SPLIT // 2 - 1 : TS_ZERO_SPLIT], 0.0)
@@ -68,8 +68,9 @@ def tile_attend_maxsim_ts_kernel(tc, qT, k_words, k_scales, ts, offs, out):
 
         halves = [offsets[:, h * LIST_COLS // 2 : (h + 1) * LIST_COLS // 2] for h in range(2)]
 
-        ts_first = sb.tile([P, HALF], F32, name="ts_first", align_bytes=64)
-        nc.vector.tensor_copy(ts_first[:], ts_pool[:].indirect(halves[0]))
+        ts_listed = [sb.tile([P, HALF], F32, name="ts_listed%d" % h, align_bytes=64) for h in range(2)]
+        for h in range(2):
+            nc.vector.tensor_copy(ts_listed[h][:], ts_pool[:].indirect(halves[h]))
 
         scales_listed = sb.tile([P, SLOTS // 4], I32, name="scales_listed", align_bytes=64)
         for h in range(2):
@@ -77,10 +78,6 @@ def tile_attend_maxsim_ts_kernel(tc, qT, k_words, k_scales, ts, offs, out):
                 scales_listed[:, h * HALF // 4 : (h + 1) * HALF // 4].bitcast(U8),
                 scale_pool[:].bitcast(U8).indirect(halves[h]),
             )
-
-        ts_second = shared.tile([P, HALF], F32, name="ts_second", align_bytes=64, offset=POOL + 4 * QUERIES)
-        nc.vector.tensor_copy(ts_second[:], ts_pool[:].indirect(halves[1]))
-        ts_listed = [ts_first, ts_second]
 
         q_grouped = shared.tile([P, QUERIES, PACK], BF16, name="q_grouped", align_bytes=64, offset=0)
         nc.scalar.copy(q_grouped[:], q_raw[:].rearrange("p j w -> p w j"))
@@ -91,11 +88,10 @@ def tile_attend_maxsim_ts_kernel(tc, qT, k_words, k_scales, ts, offs, out):
         )
 
         first, second, both = slice(0, HALF // 4), slice(HALF // 4, SLOTS // 4), slice(0, SLOTS // 4)
-        for quad, at in [(0, first), (1, first), (2, both), (3, both), (0, second), (1, second)]:
+        for quad, at in [(q, first) for q in range(3)] + [(3, both)] + [(q, second) for q in range(3)]:
             nc.sync.dma_start(
                 planes[32 * quad : 32 * quad + 4, at],
                 scales_listed[SCALE_ROW + 16 * quad : SCALE_ROW + 16 * quad + 16 : 4, at],
-                max_dma_last_dim=512,
             )
         key_scales = planes[:, 0 : SLOTS // 4].bitcast(U8)
 

@@ -43,10 +43,10 @@ def tile_attend_maxsim_ts_kernel(tc, qT, k_words, k_scales, ts, offs, out):
         ps = ctx.enter_context(tc.psum_pool(name="ps", bufs=1))
 
         offsets = sb.tile([P, LIST_COLS], U16, name="offsets")
-        ts_pool = sb.tile([P, POOL], F32, name="ts_pool", align_bytes=64)
-        q_raw = sb.tile([P, PACK, QUERIES], F32, name="q_raw", align_bytes=64)
-        word_pool = sb.tile([P, POOL], I32, name="word_pool", align_bytes=64)
-        scale_pool = shared.tile([P, POOL // 4], I32, name="scale_pool", align_bytes=64, offset=1024)
+        ts_pool = sb.tile([P, POOL], F32, name="ts_pool", align_bytes=256)
+        q_raw = sb.tile([P, PACK, QUERIES], F32, name="q_raw", align_bytes=256)
+        word_pool = sb.tile([P, POOL], I32, name="word_pool", align_bytes=256)
+        scale_pool = shared.tile([P, POOL // 4], I32, name="scale_pool", align_bytes=256, offset=1024)
         planes = sb.tile([P, (SLOTS + QUERIES) // 4], I32, name="planes", align_bytes=64)
         identity = sb.tile([P, P], F32, name="identity", align_bytes=64)
 

from contextlib import ExitStack

import concourse.mybir as mybir
from concourse.masks import make_identity

F32 = mybir.dt.float32
BF16 = mybir.dt.bfloat16
I32 = mybir.dt.int32
U32 = mybir.dt.uint32
U16 = mybir.dt.uint16
U8 = mybir.dt.uint8
FP8X4 = mybir.dt.float8_e4m3fn_x4
MULT = mybir.AluOpType.mult
MAX = mybir.AluOpType.max
AXIS_X = mybir.AxisListType.X
COPY = mybir.ActivationFunctionType.Copy

P = 128
PACK = 4
POOL = 4096
SLOTS = 1024
QUERIES = 128
SEG = 128
PASSAGES = SLOTS // SEG
LIST_COLS = SLOTS // 16
HALF = SLOTS // 2
PIECES = (3, 3, 2)
TURNED = (2, 4)
TS_ROW = P - 1
SCALE_ROW = 32
SCALE_ZERO_SPLIT = 416
TS_ZERO_SPLIT = 2016

FLOPS = 2 * QUERIES * SLOTS * P * PACK
BYTES = P * POOL * 4 + 16 * POOL + P * PACK * QUERIES * 4 + POOL * 4 + P * LIST_COLS * 2 + QUERIES * PASSAGES * 4


def tile_attend_maxsim_ts_kernel(tc, qT, k_words, k_scales, ts, offs, out):
    nc = tc.nc
    with ExitStack() as ctx:
        sb = ctx.enter_context(tc.tile_pool(name="sb", bufs=1))
        shared = ctx.enter_context(tc.tile_pool(name="shared", bufs=1))
        ps = ctx.enter_context(tc.psum_pool(name="ps", bufs=1))

        offsets = sb.tile([P, LIST_COLS], U16, name="offsets")
        ts_pool = sb.tile([P, POOL], F32, name="ts_pool", align_bytes=256)
        q_raw = sb.tile([P, PACK, QUERIES], F32, name="q_raw", align_bytes=256)
        word_pool = sb.tile([P, POOL], I32, name="word_pool", align_bytes=256)
        scale_pool = shared.tile([P, POOL // 4], I32, name="scale_pool", align_bytes=256, offset=1024)
        planes = sb.tile([P, (SLOTS + QUERIES) // 4], I32, name="planes", align_bytes=64)
        identity = sb.tile([P, P], F32, name="identity", align_bytes=64)

        nc.vector.memset(scale_pool[:, 0 : SCALE_ZERO_SPLIT // 2 - 1], 0)
        nc.vector.memset(scale_pool[:, SCALE_ZERO_SPLIT // 2 - 1 : SCALE_ZERO_SPLIT], 0)
        nc.gpsimd.memset(scale_pool[:, SCALE_ZERO_SPLIT:], 0)

        nc.scalar.dma_start(ts_pool[TS_ROW:P, :], ts[0:1, :])
        nc.sync.dma_start(q_raw[:], qT[0].rearrange("(p j) w -> p j w", j=PACK))
        nc.sync.dma_start(offsets[:], offs)
        nc.scalar.dma_start(scale_pool[SCALE_ROW : SCALE_ROW + 64 : 4, :], k_scales[0].bitcast(I32))
        nc.scalar.dma_start(word_pool[:], k_words[0].rearrange("p n t -> p (n t)").bitcast(I32))

        nc.vector.memset(ts_pool[0:TS_ROW, 0 : TS_ZERO_SPLIT // 2 - 1], 0.0)
        nc.vector.memset(ts_pool[0:TS_ROW, TS_ZERO_SPLIT // 2 - 1 : TS_ZERO_SPLIT], 0.0)
        nc.gpsimd.memset(ts_pool[0:TS_ROW, TS_ZERO_SPLIT:POOL], 0.0)
        make_identity(nc, identity[:])
        nc.gpsimd.memset(planes[:], 0)

        halves = [offsets[:, h * LIST_COLS // 2 : (h + 1) * LIST_COLS // 2] for h in range(2)]

        ts_listed = [sb.tile([P, HALF], F32, name="ts_listed%d" % h, align_bytes=64) for h in range(2)]
        for h in range(2):
            nc.vector.tensor_copy(ts_listed[h][:], ts_pool[:].indirect(halves[h]))

        scales_listed = sb.tile([P, SLOTS // 4], I32, name="scales_listed", align_bytes=64)
        for h in range(2):
            nc.vector.tensor_copy(
                scales_listed[:, h * HALF // 4 : (h + 1) * HALF // 4].bitcast(U8),
                scale_pool[:].bitcast(U8).indirect(halves[h]),
            )

        q_grouped = shared.tile([P, QUERIES, PACK], BF16, name="q_grouped", align_bytes=64, offset=0)
        nc.scalar.copy(q_grouped[:], q_raw[:].rearrange("p j w -> p w j"))
        q_words = shared.tile([P, QUERIES], U32, name="q_words", align_bytes=64, offset=POOL)
        q_scales = planes[:, SLOTS // 4 :].bitcast(U8)
        nc.vector.quantize_mx(
            out=q_words[:].bitcast(FP8X4), scales=q_scales, in_=q_grouped[:].rearrange("p w j -> p (w j)")
        )

        first, second, both = slice(0, HALF // 4), slice(HALF // 4, SLOTS // 4), slice(0, SLOTS // 4)
        for quad, at in [(q, first) for q in range(3)] + [(3, both)] + [(q, second) for q in range(3)]:
            nc.sync.dma_start(
                planes[32 * quad : 32 * quad + 4, at],
                scales_listed[SCALE_ROW + 16 * quad : SCALE_ROW + 16 * quad + 16 : 4, at],
            )
        key_scales = planes[:, 0 : SLOTS // 4].bitcast(U8)

        ts_cols = []
        for h in range(2):
            turned = ps.tile([P, 4, SEG], F32, name="turned%d" % h, tag="bank%d" % (5 + h))
            for j in range(4):
                nc.tensor.transpose(turned[:, j, :], ts_listed[h][:, j * SEG : (j + 1) * SEG], identity[:])
            c = sb.tile([P, 4], F32, name="ts_cols%d" % h, align_bytes=64)
            nc.scalar.copy(c[:], turned[:, :, TS_ROW])
            ts_cols.extend([c[:, j : j + 1] for j in range(4)])
        ts_spread = {}
        for h in range(2):
            direct = [j for j in range(4 * h, 4 * h + 4) if j not in TURNED]
            spread = ps.tile([P, 3, SEG], F32, name="spread%d" % h, tag="bank%d" % (4, 7)[h])
            for i, j in enumerate(direct):
                nc.tensor.transpose(spread[:, i, :], ts_cols[j].to_broadcast([P, P]), identity[:])
            s = sb.tile([P, 3 * SEG], F32, name="ts_spread%d" % h, align_bytes=64)
            nc.scalar.copy(s[:], spread[:].rearrange("p j s -> p (j s)"))
            for i, j in enumerate(direct):
                ts_spread.setdefault(j, (s, i * SEG))

        key_words = shared.tile([P, SLOTS], U32, name="key_words", align_bytes=64, offset=0)
        at = 0
        for count in PIECES:
            nc.vector.tensor_copy(
                key_words[:, at * SEG : (at + count) * SEG],
                word_pool[:].bitcast(U32).indirect(offsets[:, at * SEG // 16 : (at + count) * SEG // 16]),
            )
            at = at + count

        def score(acc, stationary, stationary_scale, moving, moving_scale):
            nc.tensor.matmul_mx(
                out=acc,
                lhsT=stationary.bitcast(FP8X4),
                lhsT_scale=stationary_scale,
                rhs=moving.bitcast(FP8X4),
                rhs_scale=moving_scale,
                start=True,
                stop=True,
            )

        scores = {}
        by_slot = {}
        for j, count in ((0, 1), (1, 1), (2, 1), (3, 1), (4, 1), (5, 1), (6, 2)):
            at = slice(j * SEG, (j + count) * SEG)
            acc = ps.tile([P, count * SEG], F32, name="scores%d" % j, tag="bank%d" % j)
            if j in TURNED:
                score(acc[:], key_words[:, at], key_scales[:, at], q_words[:], q_scales)
                y = sb.tile([P, QUERIES], F32, name="slot_scaled%d" % j, align_bytes=64)
                nc.scalar.activation(y[:], acc[:], COPY, scale=ts_cols[j])
                by_slot.setdefault(j, y)
            else:
                score(acc[:], q_words[:], q_scales, key_words[:, at], key_scales[:, at])
                scores.setdefault(j, acc)
        back = {}
        for j in TURNED:
            t = ps.tile([P, SEG], F32, name="back%d" % j, tag="bank%d" % j)
            nc.tensor.transpose(t[:], by_slot[j][:], identity[:])
            back.setdefault(j, t)

        best = sb.tile([P, PASSAGES], F32, name="best", align_bytes=64)
        scaled = {}

        def product(j, count):
            y = sb.tile([P, count * SEG], F32, name="scaled%d" % j, align_bytes=64)
            s, at = ts_spread[j]
            nc.vector.tensor_tensor(y[:], scores[j][:], s[:, at : at + count * SEG], MULT)
            scaled.setdefault(j, y)

        def maximum(j, count, source):
            nc.vector.tensor_reduce(
                best[:, j : j + count], source[:].rearrange("p (j s) -> p j s", s=SEG), AXIS_X, MAX
            )

        product(0, 1)
        product(1, 1)
        maximum(0, 1, scaled[0])
        product(3, 1)
        maximum(1, 1, scaled[1])
        product(5, 1)
        maximum(3, 1, scaled[3])
        product(6, 2)
        maximum(5, 1, scaled[5])
        maximum(2, 1, back[2])
        maximum(6, 2, scaled[6])
        maximum(4, 1, back[4])
        nc.sync.dma_start(out[0], best[:])
